import numpy as np
CORES = [0,1,2,3,4,5,6,7]
N = 8
COUNTS = [[0,0,0,0,0,0,256,0],[0,0,0,0,0,0,256,0],[0,0,0,0,0,0,256,0],[0,0,0,0,0,0,256,0],[0,0,0,0,0,0,256,0],[0,0,0,0,0,0,256,0],[32,32,32,32,32,32,32,32],[0,0,0,0,0,0,256,0]]
XW, YW = 256, 1824
def setup_inputs(rng):
    return {"x": rng.standard_normal((N, 128, XW), dtype=np.float32)}
def reference(x):
    y = np.full((N, 128, YW), np.nan, x.dtype)
    fill = [0] * N
    for s in range(N):
        o = 0
        for d in range(N):
            c = COUNTS[s][d]
            y[d][:, fill[d]:fill[d] + c] = x[s][:, o:o + c]
            o += c; fill[d] += c
    return {"y": y}

@@ -1,0 +1,89 @@
+from concourse.bass import DstId, RemoteDMATransfer
+
+NRANKS = 8
+XW, YW = 256, 1824
+
+SCRATCH = {
+    "stage": ("sbuf", [128, XW], "float32"),
+    "land": ("sbuf", [128, YW], "float32"),
+}
+SEMAPHORES = ["loaded", "sent", "stored"] + ["arr%d" % s for s in range(NRANKS)]
+
+
+def engines_for(n_transfers):
+    e = 16
+    while e * n_transfers > 16:
+        e //= 2
+    return e
+
+
+def calls_of(counts, s):
+    by_width = {}
+    for d in range(len(counts)):
+        if d != s and counts[s][d] > 0:
+            by_width.setdefault(counts[s][d], []).append(d)
+    calls = []
+    for w in sorted(by_width):
+        dsts = by_width[w]
+        for k in range(0, len(dsts), 16):
+            part = dsts[k:k + 16]
+            e = engines_for(len(part))
+            calls.append([(d, e, ((1 << e) - 1) << (e * i)) for i, d in enumerate(part)])
+    return calls
+
+
+def rank_program(g, core, T, topo):
+    rank = T.rank_of(core)
+    if rank is None:
+        return
+    counts = T.tables["COUNTS"]
+    n = len(counts)
+    xoff = [sum(counts[rank][:d]) for d in range(n)]
+    used = sum(counts[rank])
+
+    def yoff(d, s):
+        return sum(counts[k][d] for k in range(s))
+
+    calls = calls_of(counts, rank)
+    stores = 0
+
+    if calls:
+        g.sync.dma_start(T.stage[:, 0:used], T.x[:, 0:used]).then_inc(T.sem.loaded, 16)
+
+    own = counts[rank][rank]
+    if own:
+        o = yoff(rank, rank)
+        g.scalar.dma_start(T.y[:, o:o + own], T.x[:, xoff[rank]:xoff[rank] + own]).then_inc(T.sem.stored, 16)
+        stores += 1
+
+    sent = 0
+    if calls:
+        g.wait_ge(T.sem.loaded, 16)
+    for call in calls:
+        transfers = []
+        for d, e, m in call:
+            rid, pid, _se = topo.addr(T.cores[d])
+            w = counts[rank][d]
+            o = yoff(d, rank)
+            transfers.append(RemoteDMATransfer(
+                dst_ids=[DstId(rid=rid, pnc=pid)], dma_engine_mask=m, remote_sem=T.sem["arr%d" % rank],
+                src=T.stage[:, xoff[d]:xoff[d] + w], dst=T.land[:, o:o + w]))
+            sent += e
+        g.remote_dma_fused(transfers, local_sem=T.sem.sent)
+
+    queues = [g.sync, g.scalar]
+    for s in range(n):
+        w = counts[s][rank]
+        if s == rank or w == 0:
+            continue
+        e = [e for call in calls_of(counts, s) for d, e, m in call if d == rank][0]
+        q = queues[stores % 2]
+        o = yoff(rank, s)
+        q.wait_ge(T.sem["arr%d" % s], e)
+        q.dma_start(T.y[:, o:o + w], T.land[:, o:o + w]).then_inc(T.sem.stored, 16)
+        stores += 1
+
+    if sent:
+        g.wait_ge(T.sem.sent, sent)
+    if stores:
+        g.wait_ge(T.sem.stored, 16 * stores)

@@ -1,13 +1,13 @@
 from concourse.bass import DstId, RemoteDMATransfer
 
-NRANKS = 8
 XW, YW = 256, 1824
+MAX_RUNS = 2
 
 SCRATCH = {
     "stage": ("sbuf", [128, XW], "float32"),
     "land": ("sbuf", [128, YW], "float32"),
 }
-SEMAPHORES = ["loaded", "sent", "stored"] + ["arr%d" % s for s in range(NRANKS)]
+SEMAPHORES = ["loaded", "sent", "stored"] + ["arr%d" % r for r in range(MAX_RUNS)]
 
 
 def engines_for(n_transfers):
@@ -32,20 +32,36 @@ def calls_of(counts, s):
     return calls
 
 
+def runs_at(counts, dies, d):
+    runs = []
+    for s in range(len(counts)):
+        if counts[s][d] == 0:
+            continue
+        if runs and dies[runs[-1][-1]] == dies[s]:
+            runs[-1].append(s)
+        else:
+            runs.append([s])
+    return runs
+
+
 def rank_program(g, core, T, topo):
     rank = T.rank_of(core)
     if rank is None:
         return
     counts = T.tables["COUNTS"]
     n = len(counts)
+    dies = [topo.die(c) for c in T.cores]
     xoff = [sum(counts[rank][:d]) for d in range(n)]
     used = sum(counts[rank])
 
     def yoff(d, s):
         return sum(counts[k][d] for k in range(s))
 
+    def run_sem(d, s):
+        r = [i for i, run in enumerate(runs_at(counts, dies, d)) if s in run][0]
+        return T.sem["arr%d" % r]
+
     calls = calls_of(counts, rank)
-    stores = 0
 
     if calls:
         g.sync.dma_start(T.stage[:, 0:used], T.x[:, 0:used]).then_inc(T.sem.loaded, 16)
@@ -53,8 +69,7 @@ def rank_program(g, core, T, topo):
     own = counts[rank][rank]
     if own:
         o = yoff(rank, rank)
-        g.scalar.dma_start(T.y[:, o:o + own], T.x[:, xoff[rank]:xoff[rank] + own]).then_inc(T.sem.stored, 16)
-        stores += 1
+        g.scalar.dma_start(T.land[:, o:o + own], T.x[:, xoff[rank]:xoff[rank] + own]).then_inc(run_sem(rank, rank), 16)
 
     sent = 0
     if calls:
@@ -66,21 +81,24 @@ def rank_program(g, core, T, topo):
             w = counts[rank][d]
             o = yoff(d, rank)
             transfers.append(RemoteDMATransfer(
-                dst_ids=[DstId(rid=rid, pnc=pid)], dma_engine_mask=m, remote_sem=T.sem["arr%d" % rank],
+                dst_ids=[DstId(rid=rid, pnc=pid)], dma_engine_mask=m, remote_sem=run_sem(d, rank),
                 src=T.stage[:, xoff[d]:xoff[d] + w], dst=T.land[:, o:o + w]))
             sent += e
         g.remote_dma_fused(transfers, local_sem=T.sem.sent)
 
-    queues = [g.sync, g.scalar]
-    for s in range(n):
-        w = counts[s][rank]
-        if s == rank or w == 0:
-            continue
-        e = [e for call in calls_of(counts, s) for d, e, m in call if d == rank][0]
-        q = queues[stores % 2]
-        o = yoff(rank, s)
-        q.wait_ge(T.sem["arr%d" % s], e)
-        q.dma_start(T.y[:, o:o + w], T.land[:, o:o + w]).then_inc(T.sem.stored, 16)
+    stores = 0
+    for r, run in enumerate(runs_at(counts, dies, rank)):
+        due = 0
+        for s in run:
+            if s == rank:
+                due += 16
+            else:
+                due += [e for call in calls_of(counts, s) for d, e, m in call if d == rank][0]
+        q = g.scalar if dies[run[0]] == dies[rank] else g.sync
+        lo = yoff(rank, run[0])
+        hi = yoff(rank, run[-1]) + counts[run[-1]][rank]
+        q.wait_ge(T.sem["arr%d" % r], due)
+        q.dma_start(T.y[:, lo:hi], T.land[:, lo:hi]).then_inc(T.sem.stored, 16)
         stores += 1
 
     if sent:

from concourse.bass import DstId, RemoteDMATransfer

XW, YW = 256, 1824
MAX_RUNS = 2

SCRATCH = {
    "stage": ("sbuf", [128, XW], "float32"),
    "land": ("sbuf", [128, YW], "float32"),
}
SEMAPHORES = ["loaded", "sent", "stored"] + ["arr%d" % r for r in range(MAX_RUNS)]


def engines_for(n_transfers):
    e = 16
    while e * n_transfers > 16:
        e //= 2
    return e


def calls_of(counts, s):
    by_width = {}
    for d in range(len(counts)):
        if d != s and counts[s][d] > 0:
            by_width.setdefault(counts[s][d], []).append(d)
    calls = []
    for w in sorted(by_width):
        dsts = by_width[w]
        for k in range(0, len(dsts), 16):
            part = dsts[k:k + 16]
            e = engines_for(len(part))
            calls.append([(d, e, ((1 << e) - 1) << (e * i)) for i, d in enumerate(part)])
    return calls


def runs_at(counts, dies, d):
    runs = []
    for s in range(len(counts)):
        if counts[s][d] == 0:
            continue
        if runs and dies[runs[-1][-1]] == dies[s]:
            runs[-1].append(s)
        else:
            runs.append([s])
    return runs


def rank_program(g, core, T, topo):
    rank = T.rank_of(core)
    if rank is None:
        return
    counts = T.tables["COUNTS"]
    n = len(counts)
    dies = [topo.die(c) for c in T.cores]
    xoff = [sum(counts[rank][:d]) for d in range(n)]
    used = sum(counts[rank])

    def yoff(d, s):
        return sum(counts[k][d] for k in range(s))

    def run_sem(d, s):
        r = [i for i, run in enumerate(runs_at(counts, dies, d)) if s in run][0]
        return T.sem["arr%d" % r]

    calls = calls_of(counts, rank)

    if calls:
        g.sync.dma_start(T.stage[:, 0:used], T.x[:, 0:used]).then_inc(T.sem.loaded, 16)

    own = counts[rank][rank]
    if own:
        o = yoff(rank, rank)
        g.scalar.dma_start(T.land[:, o:o + own], T.x[:, xoff[rank]:xoff[rank] + own]).then_inc(run_sem(rank, rank), 16)

    sent = 0
    if calls:
        g.wait_ge(T.sem.loaded, 16)
    for call in calls:
        transfers = []
        for d, e, m in call:
            rid, pid, _se = topo.addr(T.cores[d])
            w = counts[rank][d]
            o = yoff(d, rank)
            transfers.append(RemoteDMATransfer(
                dst_ids=[DstId(rid=rid, pnc=pid)], dma_engine_mask=m, remote_sem=run_sem(d, rank),
                src=T.stage[:, xoff[d]:xoff[d] + w], dst=T.land[:, o:o + w]))
            sent += e
        g.remote_dma_fused(transfers, local_sem=T.sem.sent)

    stores = 0
    for r, run in enumerate(runs_at(counts, dies, rank)):
        due = 0
        for s in run:
            if s == rank:
                due += 16
            else:
                due += [e for call in calls_of(counts, s) for d, e, m in call if d == rank][0]
        q = g.scalar if dies[run[0]] == dies[rank] else g.sync
        lo = yoff(rank, run[0])
        hi = yoff(rank, run[-1]) + counts[run[-1]][rank]
        q.wait_ge(T.sem["arr%d" % r], due)
        q.dma_start(T.y[:, lo:hi], T.land[:, lo:hi]).then_inc(T.sem.stored, 16)
        stores += 1

    if sent:
        g.wait_ge(T.sem.sent, sent)
    if stores:
        g.wait_ge(T.sem.stored, 16 * stores)
